import numpy as np
import ml_dtypes


def mxq(x, axis, fmt="e4m3"):
    dtype, down = {"e4m3": (ml_dtypes.float8_e4m3fn, 7), "e5m2": (ml_dtypes.float8_e5m2, 14)}[fmt]
    v = np.moveaxis(np.asarray(x, np.float32).astype(ml_dtypes.bfloat16).astype(np.float64), axis, -1)
    blocks = v.reshape(v.shape[:-1] + (-1, 32))
    amax = np.abs(blocks).max(-1, keepdims=True)
    byte = np.maximum(np.where(amax > 0, np.frexp(amax)[1] - 1 + 127, 0) - down, 1)
    scale = np.exp2(byte - 127.0)
    codes = (blocks / scale).astype(np.float32).astype(dtype).astype(np.float64)
    return np.moveaxis((codes * scale).reshape(v.shape), -1, axis)


WIDE = False


def mx_kscale(k):
    if not WIDE:
        return np.ones(k)
    levels = np.array([10, -10, 5, -5, 0])
    if k % 512:
        return np.exp2(np.random.permutation(np.resize(levels, k // 32))).repeat(32)
    a = np.empty((k // 512, 16))
    for p in range(k // 512):
        a[p, :8] = np.random.permutation(np.resize(levels, 8))
        for g in range(8):
            far = levels[np.abs(levels - a[p, g]) >= 10]
            a[p, g + 8] = far[np.random.randint(len(far))]
    return np.exp2(a.ravel()).repeat(32)


def f64(x):
    return np.asarray(x).astype(np.float64)


def striped(idx):
    return np.tile(np.asarray(idx).reshape(-1, 16).T, (8, 1)).astype(np.uint16)


def unstriped(offs):
    return offs[:16].T.reshape(-1).astype(np.int64)


def striped8(idx):
    return np.asarray(idx).reshape(8, -1, 16).transpose(0, 2, 1).reshape(128, -1).astype(np.uint16)


def unstriped8(offs):
    return offs.reshape(8, 16, -1).transpose(0, 2, 1).reshape(8, -1).astype(np.int64)


def pick8(x, idx, run):
    r = np.arange(len(x))
    return x[r[:, None], idx[r % (8 * run) // run]]


E2M1 = np.array([0.0, 0.5, 1.0, 1.5, 2.0, 3.0, 4.0, 6.0, -0.0, -0.5, -1.0, -1.5, -2.0, -3.0, -4.0, -6.0])


def pack_weight(w, fmt):
    k, n = w.shape
    w = f64(np.asarray(w, np.float32).astype(ml_dtypes.bfloat16)).reshape(k // 32, 32, n)
    amax = np.abs(w).max(1)
    if fmt == "e4m3":
        byte = np.frexp(amax)[1] - 1 + 127 - 7
    else:
        mant, ex = np.frexp(amax / 6.0)
        byte = np.where(mant > 0.5, ex, ex - 1) + 127
    byte = np.clip(np.where(amax > 0, byte, 1), 1, 254)
    scaled = (w * np.exp2(127.0 - byte)[:, None, :]).reshape(k, n).astype(np.float32)
    by_word = np.ascontiguousarray(scaled.reshape(k // 512, 128, 4, n).transpose(0, 1, 3, 2))
    if fmt == "e4m3":
        words = by_word.astype(ml_dtypes.float8_e4m3fn).view(np.uint8)
    else:
        c = by_word.astype(ml_dtypes.float4_e2m1fn).view(np.uint8) & 0xF
        words = (c[..., 0::2] | (c[..., 1::2] << 4)).reshape(k // 512, 128, 2 * n)
    return np.ascontiguousarray(words), np.ascontiguousarray(byte.astype(np.uint8).reshape(k // 512, 16, n))


def unpack_weight(words, scales, fmt):
    g, _, n = scales.shape
    words = np.ascontiguousarray(words).reshape(g, 128, n, -1)
    if fmt == "e4m3":
        vals = words.view(ml_dtypes.float8_e4m3fn).astype(np.float64)
    else:
        nib = np.empty((g, 128, n, 4), np.uint8)
        nib[..., 0::2] = words & 0xF
        nib[..., 1::2] = words >> 4
        vals = E2M1[nib]
    vals = vals * np.repeat(np.exp2(scales.astype(np.float64) - 127.0), 8, axis=1)[..., None]
    return vals.transpose(0, 1, 3, 2).reshape(g * 512, n)


K, J, R, T, F, C, O, N, S, Z = 512, 256, 512, 1024, 1024, 512, 128, 256, 1024, 1024


def setup_inputs():
    n = np.random.standard_normal
    idx = np.random.permutation(T)[:J]
    idx2 = np.stack([np.random.permutation(F)[:R] for _ in range(8)])
    idx3 = np.random.permutation(C)[:J]
    idx4 = np.random.permutation(C)[:O]
    idx5 = np.stack([np.random.permutation(C)[:O] for _ in range(8)])
    idx6 = np.random.permutation(S)[:N]
    idx7 = np.stack([np.random.permutation(Z)[:N] for _ in range(8)])
    fk = mx_kscale(K)
    fr = mx_kscale(R)
    xtp = pack_weight(n((K, T)) * fk[:, None], "e2m1")
    return {
        "xt_words": xtp[0],
        "xt_scales": xtp[1],
        "ua": (np.random.randint(-7, 8, (K, F)).astype(np.float64)).astype(np.float32),
        "ha": ((np.random.randint(8, 25, (K, 1)) / 1024.0) / fk[:, None]).astype(np.float32),
        "sa": (np.random.uniform(0.5, 1.6, (R, 1)) * fr[:, None]).astype(np.float32),
        "sb": (np.random.uniform(0.5, 1.6, (R, 1)) * fr[:, None]).astype(np.float32),
        "va": (np.random.randint(-7, 8, (R, S)).astype(np.float64)).astype(np.float32),
        "vb": (np.random.randint(-7, 8, (R, Z)).astype(np.float64)).astype(np.float32),
        "ea": ((np.random.randint(10, 25, (R, 1)) / 1024.0) / fr[:, None]).astype(np.float32),
        "eb": ((np.random.randint(4, 13, (R, 1)) / 1024.0) / fr[:, None]).astype(np.float32),
        "offs": striped(idx),
        "offs2": striped8(idx2),
        "offs3": striped(idx3),
        "offs4": striped(idx4),
        "offs5": striped8(idx5),
        "offs6": striped(idx6),
        "offs7": striped8(idx7),
    }


def reference(xt_words, xt_scales, ua, ha, sa, sb, va, vb, ea, eb, offs, offs2, offs3, offs4, offs5, offs6, offs7):
    idx = unstriped(offs)
    idx2 = unstriped8(offs2)
    idx3 = unstriped(offs3)
    idx4 = unstriped(offs4)
    idx5 = unstriped8(offs5)
    idx6 = unstriped(offs6)
    idx7 = unstriped8(offs7)
    xtu = unpack_weight(xt_words, xt_scales, "e2m1")
    wc = pick8(f64(ua), idx2, 64) * f64(ha)
    wcq = mxq(wc, 0, "e4m3")
    xtidxg = xtu[:, idx]
    a = wcq.T @ xtidxg
    pw = np.zeros((R, C))
    pw[:, idx3] = a
    hid = np.abs(pw[:, idx4] * f64(sa) - pick8(pw, idx5, 64) * f64(sb))
    vc = f64(va)[:, idx6] * f64(ea) + pick8(f64(vb), idx7, 64) * f64(eb)
    vcq = mxq(vc, 0, "e4m3")
    hidq = mxq(hid, 0, "e4m3")
    y = vcq.T @ hidq
    return y

@@ -1,0 +1,223 @@
+from contextlib import ExitStack
+
+import concourse.mybir as mybir
+
+K, J, R, T, F, C, O, N = 512, 256, 512, 1024, 1024, 512, 128, 256
+FLOPS = 2 * K * R * J + 2 * R * N * O
+
+F32 = mybir.dt.float32
+BF16 = mybir.dt.bfloat16
+I32 = mybir.dt.int32
+U32 = mybir.dt.uint32
+U16 = mybir.dt.uint16
+U8 = mybir.dt.uint8
+FP8X4 = mybir.dt.float8_e4m3fn_x4
+FP4X4 = mybir.dt.float4_e2m1fn_x4
+COPY = mybir.ActivationFunctionType.Copy
+ABS = mybir.ActivationFunctionType.Abs
+ADD = mybir.AluOpType.add
+SUB = mybir.AluOpType.subtract
+
+P = 128
+PACK = 4
+
+
+def tile_picked_tokens_codes_one_boardmixed_basedetail_plain_kernel(
+    tc, xt_words, xt_scales, ua, ha, sa, sb, va, vb, ea, eb, offs, offs2, offs3, offs4, offs5, offs6, offs7, out
+):
+    nc = tc.nc
+    with ExitStack() as ctx:
+        lists = ctx.enter_context(tc.tile_pool(name="lists", bufs=1))
+        keep = ctx.enter_context(tc.tile_pool(name="keep", bufs=1))
+        psum = ctx.enter_context(tc.psum_pool(name="psum", bufs=1))
+
+        def load_list(src, name):
+            tile = lists.tile(list(src.shape), U16, name=name)
+            nc.sync.dma_start(tile[:], src)
+            return tile
+
+        def load_rows(src, t, name):
+            tile = keep.tile([P, src.shape[1]], F32, name=name, tag=name)
+            nc.sync.dma_start(out=tile[:], in_=src.rearrange("(p t) c -> t p c", t=PACK)[t])
+            return tile
+
+        def load_column(queue, src, name):
+            tile = keep.tile([P, PACK], F32, name=name)
+            queue.dma_start(out=tile[:], in_=src.rearrange("(p t) o -> p (t o)", t=PACK))
+            return tile
+
+        ua_rows = [load_rows(ua, 0, "ua0")]
+        list2 = load_list(offs2, "list2")
+        ha_col = load_column(nc.scalar, ha, "ha_col")
+        ua_rows.append(load_rows(ua, 1, "ua1"))
+        list1 = load_list(offs, "list1")
+        ua_rows.append(load_rows(ua, 2, "ua2"))
+        ua_rows.append(load_rows(ua, 3, "ua3"))
+        words_all = keep.tile([P, 2 * T], U8, name="words_all", align_bytes=64)
+        nc.sync.dma_start(out=words_all[:], in_=xt_words[0])
+
+        scale_stage = keep.tile([4, 4, T], U8, name="scale_stage")
+        nc.gpsimd.dma_start(
+            out=scale_stage[:].bitcast(I32), in_=xt_scales[0].bitcast(I32).rearrange("(q r) c -> r q c", r=4)
+        )
+        ea_col = load_column(nc.gpsimd, ea, "ea_col")
+        eb_col = load_column(nc.gpsimd, eb, "eb_col")
+        sa_col = load_column(nc.gpsimd, sa, "sa_col")
+        sb_col = load_column(nc.gpsimd, sb, "sb_col")
+
+        va_rows, vb_rows = [], []
+        list6 = load_list(offs6, "list6")
+        va_rows.append(load_rows(va, 0, "va0"))
+        list7 = load_list(offs7, "list7")
+        vb_rows.append(load_rows(vb, 0, "vb0"))
+        list3 = load_list(offs3, "list3")
+        va_rows.append(load_rows(va, 1, "va1"))
+        list4 = load_list(offs4, "list4")
+        vb_rows.append(load_rows(vb, 1, "vb1"))
+        list5 = load_list(offs5, "list5")
+        va_rows.append(load_rows(va, 2, "va2"))
+        vb_rows.append(load_rows(vb, 2, "vb2"))
+        vb_rows.append(load_rows(vb, 3, "vb3"))
+        va_rows.append(load_rows(va, 3, "va3"))
+
+        scales_all = keep.tile([P, T], U8, name="scales_all", align_bytes=64)
+        nc.vector.memset(scales_all[:].bitcast(I32), 0)
+        board = [keep.tile([P, C], F32, name="board%d" % t) for t in range(PACK)]
+        for t in range(PACK):
+            nc.vector.memset(board[t][:], 0.0)
+        for q in range(4):
+            nc.vector.tensor_copy(
+                out=scales_all[32 * q : 32 * q + 4, :].bitcast(I32), in_=scale_stage[:, q, :].bitcast(I32)
+            )
+        x_scales = keep.tile([P, J], U8, name="x_scales", align_bytes=64)
+        nc.vector.tensor_copy(out=x_scales[:], in_=scales_all[:].indirect(list1[:]))
+        x_words = keep.tile([P, 2 * J], U8, name="x_words", align_bytes=64)
+        nc.vector.tensor_copy(out=x_words[:].bitcast(U16), in_=words_all[:].bitcast(U16).indirect(list1[:]))
+
+        half = R // 2
+        wc_half = [keep.tile([P, PACK, half], BF16, name="wc_half%d" % h) for h in range(2)]
+        for j in range(PACK):
+            for h in range(2):
+                nc.scalar.activation(
+                    out=wc_half[h][:, j, :],
+                    in_=ua_rows[j][:].indirect(list2[:, h * half // 16 : (h + 1) * half // 16]),
+                    func=COPY,
+                    scale=ha_col[:, j : j + 1],
+                )
+
+        wc_grouped = keep.tile([P, PACK, P, PACK], BF16, name="wc_grouped", align_bytes=64)
+        nc.vector.tensor_copy(
+            out=wc_grouped[:, :, 0:64, :], in_=wc_half[0][:].rearrange("p j (m t) -> p t m j", t=PACK)
+        )
+        a_rows = []
+        for t in range(PACK):
+            nc.vector.tensor_copy(
+                out=wc_grouped[:, t, 64:128, :],
+                in_=wc_half[1][:].rearrange("p j (m t) -> p t m j", t=PACK)[:, t, :, :],
+            )
+        for t in range(PACK):
+            wc_codes = keep.tile([P, P], U32, name="wc_codes%d" % t, align_bytes=64)
+            wc_scales = keep.tile([P, P], U8, name="wc_scales%d" % t, align_bytes=64)
+            nc.vector.quantize_mx(
+                out=wc_codes[:].bitcast(FP8X4),
+                scales=wc_scales[:],
+                in_=wc_grouped[:, t, :, :].rearrange("p m j -> p (m j)"),
+            )
+            a_psum = psum.tile([P, J], F32, name="a_psum%d" % t)
+            nc.tensor.matmul_mx(
+                out=a_psum[:],
+                lhsT=wc_codes[:].bitcast(FP8X4),
+                lhsT_scale=wc_scales[:],
+                rhs=x_words[:].bitcast(FP4X4),
+                rhs_scale=x_scales[:],
+                start=True,
+                stop=True,
+            )
+            a_sb = keep.tile([P, J], F32, name="a_rows%d" % t)
+            nc.scalar.copy(out=a_sb[:], in_=a_psum[:])
+            a_rows.append(a_sb)
+
+        for t in range(PACK):
+            nc.vector.tensor_copy(out=board[t][:].indirect(list3[:]), in_=a_rows[t][:])
+
+        base = [keep.tile([P, PACK, P], F32, name="base%d" % h) for h in range(2)]
+        detail = keep.tile([P, PACK, N], F32, name="detail")
+        diff = keep.tile([P, PACK, O], F32, name="diff")
+
+        def fetch_base(t):
+            for h in range(2):
+                nc.scalar.activation(
+                    out=base[h][:, t, :],
+                    in_=va_rows[t][:].indirect(list6[:, 8 * h : 8 * (h + 1)]),
+                    func=COPY,
+                    scale=ea_col[:, t : t + 1],
+                )
+
+        def fetch_detail(t):
+            nc.scalar.activation(
+                out=detail[:, t, :], in_=vb_rows[t][:].indirect(list7[:]), func=COPY, scale=eb_col[:, t : t + 1]
+            )
+
+        def read_board(t, tag):
+            picked = keep.tile([P, 2, O], F32, name="picked%d" % t, tag=tag)
+            nc.scalar.activation(
+                out=picked[:, 0, :], in_=board[t][:].indirect(list4[:]), func=COPY, scale=sa_col[:, t : t + 1]
+            )
+            nc.scalar.activation(
+                out=picked[:, 1, :], in_=board[t][:].indirect(list5[:]), func=COPY, scale=sb_col[:, t : t + 1]
+            )
+            nc.vector.tensor_tensor(out=diff[:, t, :], in0=picked[:, 0, :], in1=picked[:, 1, :], op=SUB)
+
+        fetch_base(0)
+        fetch_detail(0)
+        fetch_base(1)
+        fetch_detail(1)
+        read_board(0, "vb1")
+        fetch_base(2)
+        read_board(1, "va2")
+        fetch_detail(2)
+        fetch_detail(3)
+        read_board(2, "vb3")
+        fetch_base(3)
+        read_board(3, "va3")
+
+        vc_grouped = keep.tile([P, N * PACK], BF16, name="vc_grouped", align_bytes=64)
+        vc_codes = keep.tile([P, N], U32, name="vc_codes", align_bytes=64)
+        vc_scales = keep.tile([P, N], U8, name="vc_scales", align_bytes=64)
+        for h in range(2):
+            nc.vector.tensor_tensor(
+                out=vc_grouped[:, 512 * h : 512 * (h + 1)].rearrange("p (c i t) -> p c t i", i=4, t=PACK),
+                in0=base[h][:].rearrange("p t (c i) -> p c t i", i=4),
+                in1=detail[:, :, P * h : P * (h + 1)].rearrange("p t (c i) -> p c t i", i=4),
+                op=ADD,
+            )
+        nc.vector.quantize_mx(out=vc_codes[:].bitcast(FP8X4), scales=vc_scales[:], in_=vc_grouped[:])
+
+        hid_grouped = keep.tile([P, O * PACK], BF16, name="hid_grouped", align_bytes=64)
+        nc.scalar.activation(
+            out=hid_grouped[:].rearrange("p (c i t) -> p c t i", i=4, t=PACK),
+            in_=diff[:].rearrange("p t (c i) -> p c t i", i=4),
+            func=ABS,
+        )
+        hid_codes = keep.tile([P, O], U32, name="hid_codes", align_bytes=64)
+        hid_scales = keep.tile([P, O], U8, name="hid_scales", align_bytes=64)
+        nc.vector.quantize_mx(out=hid_codes[:].bitcast(FP8X4), scales=hid_scales[:], in_=hid_grouped[:])
+
+        for h in range(2):
+            y_psum = psum.tile([P, O], F32, name="y_psum%d" % h)
+            nc.tensor.matmul_mx(
+                out=y_psum[:],
+                lhsT=vc_codes[:, P * h : P * (h + 1)].bitcast(FP8X4),
+                lhsT_scale=vc_scales[:, P * h : P * (h + 1)],
+                rhs=hid_codes[:].bitcast(FP8X4),
+                rhs_scale=hid_scales[:],
+                start=True,
+                stop=True,
+            )
+            y_sb = keep.tile([P, O], F32, name="y_rows%d" % h)
+            if h == 0:
+                nc.vector.tensor_copy(out=y_sb[:], in_=y_psum[:])
+                nc.sync.dma_start(out=out[P * h : P * (h + 1), :], in_=y_sb[:])
+            else:
+                nc.scalar.copy(out=y_sb[:], in_=y_psum[:])
+                nc.scalar.dma_start(out=out[P * h : P * (h + 1), :], in_=y_sb[:])

@@ -17,6 +17,8 @@ COPY = mybir.ActivationFunctionType.Copy
 ABS = mybir.ActivationFunctionType.Abs
 ADD = mybir.AluOpType.add
 SUB = mybir.AluOpType.subtract
+MULT = mybir.AluOpType.mult
+MAX = mybir.AluOpType.max
 
 P = 128
 PACK = 4
@@ -51,34 +53,38 @@ def tile_picked_tokens_codes_one_boardmixed_basedetail_plain_kernel(
         ha_col = load_column(nc.scalar, ha, "ha_col")
         ua_rows.append(load_rows(ua, 1, "ua1"))
         list1 = load_list(offs, "list1")
-        ua_rows.append(load_rows(ua, 2, "ua2"))
-        ua_rows.append(load_rows(ua, 3, "ua3"))
-        words_all = keep.tile([P, 2 * T], U8, name="words_all", align_bytes=64)
-        nc.sync.dma_start(out=words_all[:], in_=xt_words[0])
-
         scale_stage = keep.tile([4, 4, T], U8, name="scale_stage")
-        nc.gpsimd.dma_start(
+        nc.sync.dma_start(
             out=scale_stage[:].bitcast(I32), in_=xt_scales[0].bitcast(I32).rearrange("(q r) c -> r q c", r=4)
         )
-        ea_col = load_column(nc.gpsimd, ea, "ea_col")
-        eb_col = load_column(nc.gpsimd, eb, "eb_col")
-        sa_col = load_column(nc.gpsimd, sa, "sa_col")
-        sb_col = load_column(nc.gpsimd, sb, "sb_col")
+        ua_rows.append(load_rows(ua, 2, "ua2"))
+        ua_rows.append(load_rows(ua, 3, "ua3"))
+        words_all = keep.tile([P, 2 * T], U8, name="words_all", tag="words", align_bytes=64)
+        nc.sync.dma_start(out=words_all[:], in_=xt_words[0])
 
         va_rows, vb_rows = [], []
         list6 = load_list(offs6, "list6")
+        ea_col = load_column(nc.sync, ea, "ea_col")
         va_rows.append(load_rows(va, 0, "va0"))
         list7 = load_list(offs7, "list7")
-        vb_rows.append(load_rows(vb, 0, "vb0"))
+        eb_col = load_column(nc.sync, eb, "eb_col")
         list3 = load_list(offs3, "list3")
+        vb_rows.append(load_rows(vb, 0, "vb0"))
         va_rows.append(load_rows(va, 1, "va1"))
-        list4 = load_list(offs4, "list4")
         vb_rows.append(load_rows(vb, 1, "vb1"))
+        list4 = load_list(offs4, "list4")
+        sa_col = load_column(nc.sync, sa, "sa_col")
         list5 = load_list(offs5, "list5")
+        sb_col = load_column(nc.sync, sb, "sb_col")
         va_rows.append(load_rows(va, 2, "va2"))
         vb_rows.append(load_rows(vb, 2, "vb2"))
         vb_rows.append(load_rows(vb, 3, "vb3"))
         va_rows.append(load_rows(va, 3, "va3"))
+
+        warm_in = keep.tile([P, 1], F32, name="warm_in")
+        warm_out = keep.tile([P, 1], F32, name="warm_out")
+        nc.vector.memset(warm_in[:], 0.0)
+        nc.scalar.activation(out=warm_out[:], in_=warm_in[:], func=ABS)
 
         scales_all = keep.tile([P, T], U8, name="scales_all", align_bytes=64)
         nc.vector.memset(scales_all[:].bitcast(I32), 0)
@@ -95,6 +101,7 @@ def tile_picked_tokens_codes_one_boardmixed_basedetail_plain_kernel(
         nc.vector.tensor_copy(out=x_words[:].bitcast(U16), in_=words_all[:].bitcast(U16).indirect(list1[:]))
 
         half = R // 2
+        groups = [(0, 1), (1, 2), (2, 4)]
         wc_half = [keep.tile([P, PACK, half], BF16, name="wc_half%d" % h) for h in range(2)]
         for j in range(PACK):
             for h in range(2):
@@ -104,41 +111,50 @@ def tile_picked_tokens_codes_one_boardmixed_basedetail_plain_kernel(
                     func=COPY,
                     scale=ha_col[:, j : j + 1],
                 )
+        wc_grouped = keep.tile([P, PACK, P, PACK], BF16, name="wc_grouped", tag="words", align_bytes=64)
 
-        wc_grouped = keep.tile([P, PACK, P, PACK], BF16, name="wc_grouped", align_bytes=64)
-        nc.vector.tensor_copy(
-            out=wc_grouped[:, :, 0:64, :], in_=wc_half[0][:].rearrange("p j (m t) -> p t m j", t=PACK)
-        )
-        a_rows = []
-        for t in range(PACK):
+        def weave(h, t0, t1):
             nc.vector.tensor_copy(
-                out=wc_grouped[:, t, 64:128, :],
-                in_=wc_half[1][:].rearrange("p j (m t) -> p t m j", t=PACK)[:, t, :, :],
+                out=wc_grouped[:, t0:t1, 64 * h : 64 * (h + 1), :],
+                in_=wc_half[h][:].rearrange("p j (m t) -> p t m j", t=PACK)[:, t0:t1, :, :],
             )
-        for t in range(PACK):
-            wc_codes = keep.tile([P, P], U32, name="wc_codes%d" % t, align_bytes=64)
-            wc_scales = keep.tile([P, P], U8, name="wc_scales%d" % t, align_bytes=64)
+
+        weave(0, 0, PACK)
+
+        a_psum = [psum.tile([P, J], F32, name="a_psum%d" % t) for t in range(PACK)]
+
+        def first_product(g):
+            t0, t1 = groups[g]
+            width = (t1 - t0) * P
+            wc_codes = keep.tile([P, width], U32, name="wc_codes%d" % t0, align_bytes=64)
+            wc_scales = keep.tile([P, width], U8, name="wc_scales%d" % t0, align_bytes=64)
             nc.vector.quantize_mx(
                 out=wc_codes[:].bitcast(FP8X4),
                 scales=wc_scales[:],
-                in_=wc_grouped[:, t, :, :].rearrange("p m j -> p (m j)"),
+                in_=wc_grouped[:, t0:t1, :, :].rearrange("p t m j -> p (t m j)"),
             )
-            a_psum = psum.tile([P, J], F32, name="a_psum%d" % t)
-            nc.tensor.matmul_mx(
-                out=a_psum[:],
-                lhsT=wc_codes[:].bitcast(FP8X4),
-                lhsT_scale=wc_scales[:],
-                rhs=x_words[:].bitcast(FP4X4),
-                rhs_scale=x_scales[:],
-                start=True,
-                stop=True,
-            )
-            a_sb = keep.tile([P, J], F32, name="a_rows%d" % t)
-            nc.scalar.copy(out=a_sb[:], in_=a_psum[:])
-            a_rows.append(a_sb)
+            for t in range(t0, t1):
+                cols = slice((t - t0) * P, (t - t0 + 1) * P)
+                nc.tensor.matmul_mx(
+                    out=a_psum[t][:],
+                    lhsT=wc_codes[:, cols].bitcast(FP8X4),
+                    lhsT_scale=wc_scales[:, cols],
+                    rhs=x_words[:].bitcast(FP4X4),
+                    rhs_scale=x_scales[:],
+                    start=True,
+                    stop=True,
+                )
 
-        for t in range(PACK):
-            nc.vector.tensor_copy(out=board[t][:].indirect(list3[:]), in_=a_rows[t][:])
+        weave(1, 0, 1)
+        weave(1, 1, 2)
+        first_product(0)
+        weave(1, 2, 4)
+        first_product(1)
+        first_product(2)
+
+        def put_on_board(t, copy, a_rows):
+            copy(out=a_rows, in_=a_psum[t][:])
+            nc.vector.tensor_copy(out=board[t][:].indirect(list3[:]), in_=a_rows)
 
         base = [keep.tile([P, PACK, P], F32, name="base%d" % h) for h in range(2)]
         detail = keep.tile([P, PACK, N], F32, name="detail")
@@ -168,40 +184,59 @@ def tile_picked_tokens_codes_one_boardmixed_basedetail_plain_kernel(
             )
             nc.vector.tensor_tensor(out=diff[:, t, :], in0=picked[:, 0, :], in1=picked[:, 1, :], op=SUB)
 
-        fetch_base(0)
-        fetch_detail(0)
-        fetch_base(1)
-        fetch_detail(1)
-        read_board(0, "vb1")
-        fetch_base(2)
-        read_board(1, "va2")
-        fetch_detail(2)
-        fetch_detail(3)
-        read_board(2, "vb3")
-        fetch_base(3)
-        read_board(3, "va3")
+        vc_grouped = [keep.tile([P, P, PACK], BF16, name="vc_grouped%d" % h, align_bytes=64) for h in range(2)]
+        hid_grouped = keep.tile([P, O, PACK], BF16, name="hid_grouped", align_bytes=64)
 
-        vc_grouped = keep.tile([P, N * PACK], BF16, name="vc_grouped", align_bytes=64)
-        vc_codes = keep.tile([P, N], U32, name="vc_codes", align_bytes=64)
-        vc_scales = keep.tile([P, N], U8, name="vc_scales", align_bytes=64)
-        for h in range(2):
+        def add_half(h):
             nc.vector.tensor_tensor(
-                out=vc_grouped[:, 512 * h : 512 * (h + 1)].rearrange("p (c i t) -> p c t i", i=4, t=PACK),
+                out=vc_grouped[h][:].rearrange("p (c i) t -> p c t i", i=4),
                 in0=base[h][:].rearrange("p t (c i) -> p c t i", i=4),
                 in1=detail[:, :, P * h : P * (h + 1)].rearrange("p t (c i) -> p c t i", i=4),
                 op=ADD,
             )
-        nc.vector.quantize_mx(out=vc_codes[:].bitcast(FP8X4), scales=vc_scales[:], in_=vc_grouped[:])
 
-        hid_grouped = keep.tile([P, O * PACK], BF16, name="hid_grouped", align_bytes=64)
+        fetch_base(0)
+        a_first = keep.tile([P, J], F32, name="a_first")
+        put_on_board(0, nc.vector.tensor_copy, a_first[:])
+        fetch_detail(0)
+        a_rest = keep.tile([P, PACK - 1, J], F32, name="a_rest", tag="vb0")
+        for t in range(1, PACK):
+            put_on_board(t, nc.scalar.copy, a_rest[:, t - 1, :])
+        fetch_base(1)
+        fetch_detail(1)
+        read_board(0, "picked0")
+        fetch_base(2)
+        read_board(1, "va2")
+        fetch_detail(2)
+        read_board(2, "vb2")
+        fetch_detail(3)
+        fetch_base(3)
+        add_half(0)
+        add_half(1)
+        read_board(3, "va3")
         nc.scalar.activation(
-            out=hid_grouped[:].rearrange("p (c i t) -> p c t i", i=4, t=PACK),
+            out=hid_grouped[:].rearrange("p (c i) t -> p c t i", i=4),
             in_=diff[:].rearrange("p t (c i) -> p c t i", i=4),
             func=ABS,
         )
+
+        vc_codes = keep.tile([P, N], U32, name="vc_codes", align_bytes=64)
+        vc_scales = keep.tile([P, N], U8, name="vc_scales", align_bytes=64)
         hid_codes = keep.tile([P, O], U32, name="hid_codes", align_bytes=64)
         hid_scales = keep.tile([P, O], U8, name="hid_scales", align_bytes=64)
-        nc.vector.quantize_mx(out=hid_codes[:].bitcast(FP8X4), scales=hid_scales[:], in_=hid_grouped[:])
+
+        def quantize_vc(h):
+            nc.vector.quantize_mx(
+                out=vc_codes[:, P * h : P * (h + 1)].bitcast(FP8X4),
+                scales=vc_scales[:, P * h : P * (h + 1)],
+                in_=vc_grouped[h][:].rearrange("p n t -> p (n t)"),
+            )
+
+        quantize_vc(0)
+        quantize_vc(1)
+        nc.vector.quantize_mx(
+            out=hid_codes[:].bitcast(FP8X4), scales=hid_scales[:], in_=hid_grouped[:].rearrange("p o t -> p (o t)")
+        )
 
         for h in range(2):
             y_psum = psum.tile([P, O], F32, name="y_psum%d" % h)

@@ -48,6 +48,15 @@ def tile_picked_tokens_codes_one_boardmixed_basedetail_plain_kernel(
             queue.dma_start(out=tile[:], in_=src.rearrange("(p t) o -> p (t o)", t=PACK))
             return tile
 
+        def load_weights(t):
+            pair = []
+            for src, name in ((sa, "sa%d" % t), (sb, "sb%d" % t)):
+                tile = keep.tile([P, 1], F32, name=name)
+                with nc.allow_non_contiguous_dma(reason="one value a partition"):
+                    nc.sync.dma_start(out=tile[:], in_=src.rearrange("(p t) o -> t p o", t=PACK)[t])
+                pair.append(tile)
+            return pair
+
         ua_rows = [load_rows(ua, 0, "ua0")]
         list2 = load_list(offs2, "list2")
         ha_col = load_column(nc.scalar, ha, "ha_col")
@@ -64,22 +73,24 @@ def tile_picked_tokens_codes_one_boardmixed_basedetail_plain_kernel(
 
         va_rows, vb_rows = [], []
         list6 = load_list(offs6, "list6")
-        ea_col = load_column(nc.sync, ea, "ea_col")
+        ea_col = load_column(nc.gpsimd, ea, "ea_col")
         va_rows.append(load_rows(va, 0, "va0"))
         list7 = load_list(offs7, "list7")
-        eb_col = load_column(nc.sync, eb, "eb_col")
+        eb_col = load_column(nc.gpsimd, eb, "eb_col")
         list3 = load_list(offs3, "list3")
         vb_rows.append(load_rows(vb, 0, "vb0"))
+        list4 = load_list(offs4, "list4")
+        list5 = load_list(offs5, "list5")
         va_rows.append(load_rows(va, 1, "va1"))
         vb_rows.append(load_rows(vb, 1, "vb1"))
-        list4 = load_list(offs4, "list4")
-        sa_col = load_column(nc.sync, sa, "sa_col")
-        list5 = load_list(offs5, "list5")
-        sb_col = load_column(nc.sync, sb, "sb_col")
+        weights = [load_weights(0)]
         va_rows.append(load_rows(va, 2, "va2"))
+        weights.append(load_weights(1))
         vb_rows.append(load_rows(vb, 2, "vb2"))
         vb_rows.append(load_rows(vb, 3, "vb3"))
+        weights.append(load_weights(2))
         va_rows.append(load_rows(va, 3, "va3"))
+        weights.append(load_weights(3))
 
         warm_in = keep.tile([P, 1], F32, name="warm_in")
         warm_out = keep.tile([P, 1], F32, name="warm_out")
@@ -158,6 +169,8 @@ def tile_picked_tokens_codes_one_boardmixed_basedetail_plain_kernel(
 
         base = [keep.tile([P, PACK, P], F32, name="base%d" % h) for h in range(2)]
         detail = keep.tile([P, PACK, N], F32, name="detail")
+        first = keep.tile([P, PACK, O], F32, name="first")
+        second = keep.tile([P, PACK, O], F32, name="second")
         diff = keep.tile([P, PACK, O], F32, name="diff")
 
         def fetch_base(t):
@@ -174,15 +187,16 @@ def tile_picked_tokens_codes_one_boardmixed_basedetail_plain_kernel(
                 out=detail[:, t, :], in_=vb_rows[t][:].indirect(list7[:]), func=COPY, scale=eb_col[:, t : t + 1]
             )
 
-        def read_board(t, tag):
-            picked = keep.tile([P, 2, O], F32, name="picked%d" % t, tag=tag)
+        def read_board(t):
             nc.scalar.activation(
-                out=picked[:, 0, :], in_=board[t][:].indirect(list4[:]), func=COPY, scale=sa_col[:, t : t + 1]
+                out=first[:, t, :], in_=board[t][:].indirect(list4[:]), func=COPY, scale=weights[t][0][:]
             )
             nc.scalar.activation(
-                out=picked[:, 1, :], in_=board[t][:].indirect(list5[:]), func=COPY, scale=sb_col[:, t : t + 1]
+                out=second[:, t, :], in_=board[t][:].indirect(list5[:]), func=COPY, scale=weights[t][1][:]
             )
-            nc.vector.tensor_tensor(out=diff[:, t, :], in0=picked[:, 0, :], in1=picked[:, 1, :], op=SUB)
+
+        def subtract(t0, t1):
+            nc.vector.tensor_tensor(out=diff[:, t0:t1, :], in0=first[:, t0:t1, :], in1=second[:, t0:t1, :], op=SUB)
 
         vc_grouped = [keep.tile([P, P, PACK], BF16, name="vc_grouped%d" % h, align_bytes=64) for h in range(2)]
         hid_grouped = keep.tile([P, O, PACK], BF16, name="hid_grouped", align_bytes=64)
@@ -204,16 +218,18 @@ def tile_picked_tokens_codes_one_boardmixed_basedetail_plain_kernel(
             put_on_board(t, nc.scalar.copy, a_rest[:, t - 1, :])
         fetch_base(1)
         fetch_detail(1)
-        read_board(0, "picked0")
+        read_board(0)
         fetch_base(2)
-        read_board(1, "va2")
+        read_board(1)
         fetch_detail(2)
-        read_board(2, "vb2")
         fetch_detail(3)
+        read_board(2)
+        subtract(0, 3)
         fetch_base(3)
         add_half(0)
+        read_board(3)
+        subtract(3, 4)
         add_half(1)
-        read_board(3, "va3")
         nc.scalar.activation(
             out=hid_grouped[:].rearrange("p (c i) t -> p c t i", i=4),
             in_=diff[:].rearrange("p t (c i) -> p c t i", i=4),

from contextlib import ExitStack

import concourse.mybir as mybir

K, J, R, T, F, C, O, N = 512, 256, 512, 1024, 1024, 512, 128, 256
FLOPS = 2 * K * R * J + 2 * R * N * O

F32 = mybir.dt.float32
BF16 = mybir.dt.bfloat16
I32 = mybir.dt.int32
U32 = mybir.dt.uint32
U16 = mybir.dt.uint16
U8 = mybir.dt.uint8
FP8X4 = mybir.dt.float8_e4m3fn_x4
FP4X4 = mybir.dt.float4_e2m1fn_x4
COPY = mybir.ActivationFunctionType.Copy
ABS = mybir.ActivationFunctionType.Abs
ADD = mybir.AluOpType.add
SUB = mybir.AluOpType.subtract
MULT = mybir.AluOpType.mult
MAX = mybir.AluOpType.max

P = 128
PACK = 4


def tile_picked_tokens_codes_one_boardmixed_basedetail_plain_kernel(
    tc, xt_words, xt_scales, ua, ha, sa, sb, va, vb, ea, eb, offs, offs2, offs3, offs4, offs5, offs6, offs7, out
):
    nc = tc.nc
    with ExitStack() as ctx:
        lists = ctx.enter_context(tc.tile_pool(name="lists", bufs=1))
        keep = ctx.enter_context(tc.tile_pool(name="keep", bufs=1))
        psum = ctx.enter_context(tc.psum_pool(name="psum", bufs=1))

        def load_list(src, name):
            tile = lists.tile(list(src.shape), U16, name=name)
            nc.sync.dma_start(tile[:], src)
            return tile

        def load_rows(src, t, name):
            tile = keep.tile([P, src.shape[1]], F32, name=name, tag=name)
            nc.sync.dma_start(out=tile[:], in_=src.rearrange("(p t) c -> t p c", t=PACK)[t])
            return tile

        def load_column(queue, src, name):
            tile = keep.tile([P, PACK], F32, name=name)
            queue.dma_start(out=tile[:], in_=src.rearrange("(p t) o -> p (t o)", t=PACK))
            return tile

        def load_weights(t):
            pair = []
            for src, name in ((sa, "sa%d" % t), (sb, "sb%d" % t)):
                tile = keep.tile([P, 1], F32, name=name)
                with nc.allow_non_contiguous_dma(reason="one value a partition"):
                    nc.sync.dma_start(out=tile[:], in_=src.rearrange("(p t) o -> t p o", t=PACK)[t])
                pair.append(tile)
            return pair

        ua_rows = [load_rows(ua, 0, "ua0")]
        list2 = load_list(offs2, "list2")
        ha_col = load_column(nc.scalar, ha, "ha_col")
        ua_rows.append(load_rows(ua, 1, "ua1"))
        list1 = load_list(offs, "list1")
        scale_stage = keep.tile([4, 4, T], U8, name="scale_stage")
        nc.sync.dma_start(
            out=scale_stage[:].bitcast(I32), in_=xt_scales[0].bitcast(I32).rearrange("(q r) c -> r q c", r=4)
        )
        ua_rows.append(load_rows(ua, 2, "ua2"))
        ua_rows.append(load_rows(ua, 3, "ua3"))
        words_all = keep.tile([P, 2 * T], U8, name="words_all", tag="words", align_bytes=64)
        nc.sync.dma_start(out=words_all[:], in_=xt_words[0])

        va_rows, vb_rows = [], []
        list6 = load_list(offs6, "list6")
        ea_col = load_column(nc.gpsimd, ea, "ea_col")
        va_rows.append(load_rows(va, 0, "va0"))
        list7 = load_list(offs7, "list7")
        eb_col = load_column(nc.gpsimd, eb, "eb_col")
        list3 = load_list(offs3, "list3")
        vb_rows.append(load_rows(vb, 0, "vb0"))
        list4 = load_list(offs4, "list4")
        list5 = load_list(offs5, "list5")
        va_rows.append(load_rows(va, 1, "va1"))
        vb_rows.append(load_rows(vb, 1, "vb1"))
        weights = [load_weights(0)]
        va_rows.append(load_rows(va, 2, "va2"))
        weights.append(load_weights(1))
        vb_rows.append(load_rows(vb, 2, "vb2"))
        vb_rows.append(load_rows(vb, 3, "vb3"))
        weights.append(load_weights(2))
        va_rows.append(load_rows(va, 3, "va3"))
        weights.append(load_weights(3))

        warm_in = keep.tile([P, 1], F32, name="warm_in")
        warm_out = keep.tile([P, 1], F32, name="warm_out")
        nc.vector.memset(warm_in[:], 0.0)
        nc.scalar.activation(out=warm_out[:], in_=warm_in[:], func=ABS)

        scales_all = keep.tile([P, T], U8, name="scales_all", align_bytes=64)
        nc.vector.memset(scales_all[:].bitcast(I32), 0)
        board = [keep.tile([P, C], F32, name="board%d" % t) for t in range(PACK)]
        for t in range(PACK):
            nc.vector.memset(board[t][:], 0.0)
        for q in range(4):
            nc.vector.tensor_copy(
                out=scales_all[32 * q : 32 * q + 4, :].bitcast(I32), in_=scale_stage[:, q, :].bitcast(I32)
            )
        x_scales = keep.tile([P, J], U8, name="x_scales", align_bytes=64)
        nc.vector.tensor_copy(out=x_scales[:], in_=scales_all[:].indirect(list1[:]))
        x_words = keep.tile([P, 2 * J], U8, name="x_words", align_bytes=64)
        nc.vector.tensor_copy(out=x_words[:].bitcast(U16), in_=words_all[:].bitcast(U16).indirect(list1[:]))

        half = R // 2
        groups = [(0, 1), (1, 2), (2, 4)]
        wc_half = [keep.tile([P, PACK, half], BF16, name="wc_half%d" % h) for h in range(2)]
        for j in range(PACK):
            for h in range(2):
                nc.scalar.activation(
                    out=wc_half[h][:, j, :],
                    in_=ua_rows[j][:].indirect(list2[:, h * half // 16 : (h + 1) * half // 16]),
                    func=COPY,
                    scale=ha_col[:, j : j + 1],
                )
        wc_grouped = keep.tile([P, PACK, P, PACK], BF16, name="wc_grouped", tag="words", align_bytes=64)

        def weave(h, t0, t1):
            nc.vector.tensor_copy(
                out=wc_grouped[:, t0:t1, 64 * h : 64 * (h + 1), :],
                in_=wc_half[h][:].rearrange("p j (m t) -> p t m j", t=PACK)[:, t0:t1, :, :],
            )

        weave(0, 0, PACK)

        a_psum = [psum.tile([P, J], F32, name="a_psum%d" % t) for t in range(PACK)]

        def first_product(g):
            t0, t1 = groups[g]
            width = (t1 - t0) * P
            wc_codes = keep.tile([P, width], U32, name="wc_codes%d" % t0, align_bytes=64)
            wc_scales = keep.tile([P, width], U8, name="wc_scales%d" % t0, align_bytes=64)
            nc.vector.quantize_mx(
                out=wc_codes[:].bitcast(FP8X4),
                scales=wc_scales[:],
                in_=wc_grouped[:, t0:t1, :, :].rearrange("p t m j -> p (t m j)"),
            )
            for t in range(t0, t1):
                cols = slice((t - t0) * P, (t - t0 + 1) * P)
                nc.tensor.matmul_mx(
                    out=a_psum[t][:],
                    lhsT=wc_codes[:, cols].bitcast(FP8X4),
                    lhsT_scale=wc_scales[:, cols],
                    rhs=x_words[:].bitcast(FP4X4),
                    rhs_scale=x_scales[:],
                    start=True,
                    stop=True,
                )

        weave(1, 0, 1)
        weave(1, 1, 2)
        first_product(0)
        weave(1, 2, 4)
        first_product(1)
        first_product(2)

        def put_on_board(t, copy, a_rows):
            copy(out=a_rows, in_=a_psum[t][:])
            nc.vector.tensor_copy(out=board[t][:].indirect(list3[:]), in_=a_rows)

        base = [keep.tile([P, PACK, P], F32, name="base%d" % h) for h in range(2)]
        detail = keep.tile([P, PACK, N], F32, name="detail")
        first = keep.tile([P, PACK, O], F32, name="first")
        second = keep.tile([P, PACK, O], F32, name="second")
        diff = keep.tile([P, PACK, O], F32, name="diff")

        def fetch_base(t):
            for h in range(2):
                nc.scalar.activation(
                    out=base[h][:, t, :],
                    in_=va_rows[t][:].indirect(list6[:, 8 * h : 8 * (h + 1)]),
                    func=COPY,
                    scale=ea_col[:, t : t + 1],
                )

        def fetch_detail(t):
            nc.scalar.activation(
                out=detail[:, t, :], in_=vb_rows[t][:].indirect(list7[:]), func=COPY, scale=eb_col[:, t : t + 1]
            )

        def read_board(t):
            nc.scalar.activation(
                out=first[:, t, :], in_=board[t][:].indirect(list4[:]), func=COPY, scale=weights[t][0][:]
            )
            nc.scalar.activation(
                out=second[:, t, :], in_=board[t][:].indirect(list5[:]), func=COPY, scale=weights[t][1][:]
            )

        def subtract(t0, t1):
            nc.vector.tensor_tensor(out=diff[:, t0:t1, :], in0=first[:, t0:t1, :], in1=second[:, t0:t1, :], op=SUB)

        vc_grouped = [keep.tile([P, P, PACK], BF16, name="vc_grouped%d" % h, align_bytes=64) for h in range(2)]
        hid_grouped = keep.tile([P, O, PACK], BF16, name="hid_grouped", align_bytes=64)

        def add_half(h):
            nc.vector.tensor_tensor(
                out=vc_grouped[h][:].rearrange("p (c i) t -> p c t i", i=4),
                in0=base[h][:].rearrange("p t (c i) -> p c t i", i=4),
                in1=detail[:, :, P * h : P * (h + 1)].rearrange("p t (c i) -> p c t i", i=4),
                op=ADD,
            )

        fetch_base(0)
        a_first = keep.tile([P, J], F32, name="a_first")
        put_on_board(0, nc.vector.tensor_copy, a_first[:])
        fetch_detail(0)
        a_rest = keep.tile([P, PACK - 1, J], F32, name="a_rest", tag="vb0")
        for t in range(1, PACK):
            put_on_board(t, nc.scalar.copy, a_rest[:, t - 1, :])
        fetch_base(1)
        fetch_detail(1)
        read_board(0)
        fetch_base(2)
        read_board(1)
        fetch_detail(2)
        fetch_detail(3)
        read_board(2)
        subtract(0, 3)
        fetch_base(3)
        add_half(0)
        read_board(3)
        subtract(3, 4)
        add_half(1)
        nc.scalar.activation(
            out=hid_grouped[:].rearrange("p (c i) t -> p c t i", i=4),
            in_=diff[:].rearrange("p t (c i) -> p c t i", i=4),
            func=ABS,
        )

        vc_codes = keep.tile([P, N], U32, name="vc_codes", align_bytes=64)
        vc_scales = keep.tile([P, N], U8, name="vc_scales", align_bytes=64)
        hid_codes = keep.tile([P, O], U32, name="hid_codes", align_bytes=64)
        hid_scales = keep.tile([P, O], U8, name="hid_scales", align_bytes=64)

        def quantize_vc(h):
            nc.vector.quantize_mx(
                out=vc_codes[:, P * h : P * (h + 1)].bitcast(FP8X4),
                scales=vc_scales[:, P * h : P * (h + 1)],
                in_=vc_grouped[h][:].rearrange("p n t -> p (n t)"),
            )

        quantize_vc(0)
        quantize_vc(1)
        nc.vector.quantize_mx(
            out=hid_codes[:].bitcast(FP8X4), scales=hid_scales[:], in_=hid_grouped[:].rearrange("p o t -> p (o t)")
        )

        for h in range(2):
            y_psum = psum.tile([P, O], F32, name="y_psum%d" % h)
            nc.tensor.matmul_mx(
                out=y_psum[:],
                lhsT=vc_codes[:, P * h : P * (h + 1)].bitcast(FP8X4),
                lhsT_scale=vc_scales[:, P * h : P * (h + 1)],
                rhs=hid_codes[:].bitcast(FP8X4),
                rhs_scale=hid_scales[:],
                start=True,
                stop=True,
            )
            y_sb = keep.tile([P, O], F32, name="y_rows%d" % h)
            if h == 0:
                nc.vector.tensor_copy(out=y_sb[:], in_=y_psum[:])
                nc.sync.dma_start(out=out[P * h : P * (h + 1), :], in_=y_sb[:])
            else:
                nc.scalar.copy(out=y_sb[:], in_=y_psum[:])
                nc.scalar.dma_start(out=out[P * h : P * (h + 1), :], in_=y_sb[:])
